import numpy as np
import ml_dtypes


def mxq(x, axis, fmt="e4m3"):
    dtype, down = {"e4m3": (ml_dtypes.float8_e4m3fn, 7), "e5m2": (ml_dtypes.float8_e5m2, 14)}[fmt]
    v = np.moveaxis(np.asarray(x, np.float32).astype(ml_dtypes.bfloat16).astype(np.float64), axis, -1)
    blocks = v.reshape(v.shape[:-1] + (-1, 32))
    amax = np.abs(blocks).max(-1, keepdims=True)
    byte = np.maximum(np.where(amax > 0, np.frexp(amax)[1] - 1 + 127, 0) - down, 1)
    scale = np.exp2(byte - 127.0)
    codes = (blocks / scale).astype(np.float32).astype(dtype).astype(np.float64)
    return np.moveaxis((codes * scale).reshape(v.shape), -1, axis)


WIDE = False


def mx_kscale(k):
    if not WIDE:
        return np.ones(k)
    levels = np.array([10, -10, 5, -5, 0])
    if k % 512:
        return np.exp2(np.random.permutation(np.resize(levels, k // 32))).repeat(32)
    a = np.empty((k // 512, 16))
    for p in range(k // 512):
        a[p, :8] = np.random.permutation(np.resize(levels, 8))
        for g in range(8):
            far = levels[np.abs(levels - a[p, g]) >= 10]
            a[p, g + 8] = far[np.random.randint(len(far))]
    return np.exp2(a.ravel()).repeat(32)


def f64(x):
    return np.asarray(x).astype(np.float64)


def striped(idx):
    return np.tile(idx.reshape(-1, 16).T, (8, 1)).astype(np.uint16)


def unstriped(offs):
    return offs[:16].T.reshape(-1).astype(np.int64)


E2M1 = np.array([0.0, 0.5, 1.0, 1.5, 2.0, 3.0, 4.0, 6.0, -0.0, -0.5, -1.0, -1.5, -2.0, -3.0, -4.0, -6.0])


def pack_fp4(w):
    k, n = w.shape
    w = f64(np.asarray(w, np.float32).astype(ml_dtypes.bfloat16)).reshape(k // 32, 32, n)
    amax = np.abs(w).max(1)
    mant, ex = np.frexp(amax / 6.0)
    byte = np.clip(np.where(amax > 0, np.where(mant > 0.5, ex, ex - 1) + 127, 1), 1, 254)
    scaled = (w * np.exp2(127.0 - byte)[:, None, :]).reshape(k, n).astype(np.float32)
    c = np.ascontiguousarray(scaled.reshape(k // 512, 128, 4, n).transpose(0, 1, 3, 2)).astype(ml_dtypes.float4_e2m1fn).view(np.uint8) & 0xF
    words = (c[..., 0::2] | (c[..., 1::2] << 4)).reshape(k // 512, 128, 2 * n)
    return np.ascontiguousarray(words), np.ascontiguousarray(byte.astype(np.uint8).reshape(k // 512, 16, n))


def unpack_fp4(words, scales):
    g, _, n = scales.shape
    words = np.ascontiguousarray(words).reshape(g, 128, n, 2)
    nib = np.empty((g, 128, n, 4), np.uint8)
    nib[..., 0::2] = words & 0xF
    nib[..., 1::2] = words >> 4
    vals = E2M1[nib] * np.repeat(np.exp2(scales.astype(np.float64) - 127.0), 8, axis=1)[..., None]
    return vals.transpose(0, 1, 3, 2).reshape(g * 512, n)


def sigmoid(v):
    return 1.0 / (1.0 + np.exp(-np.maximum(v, -700.0)))


K, T, S, V, N = 1024, 2048, 512, 256, 128


def setup_inputs():
    n = np.random.standard_normal
    s = mx_kscale(K)[:, None]
    packed_w1 = pack_fp4(n((K, N)) / np.sqrt(K) / s)
    packed_w2 = pack_fp4(n((K, N)) / np.sqrt(K) / s)
    packed_w3 = pack_fp4(n((K, N)) / np.sqrt(K) / s)
    return {
        "xT": (n((K, T)) * s).astype(np.float32),
        "w1_words": packed_w1[0],
        "w1_scales": packed_w1[1],
        "w2_words": packed_w2[0],
        "w2_scales": packed_w2[1],
        "w3_words": packed_w3[0],
        "w3_scales": packed_w3[1],
        "offs": striped(np.random.permutation(T)[:S]),
        "cen": striped(np.random.permutation(S)[:V]),
        "pos1": striped(np.random.permutation(S)[:V]),
        "pos2": striped(np.random.permutation(S)[:V]),
        "pos3": striped(np.random.permutation(S)[:V]),
    }


def reference(xT, w1_words, w1_scales, w2_words, w2_scales, w3_words, w3_scales, offs, cen, pos1, pos2, pos3):
    xq = mxq(f64(xT)[:, unstriped(offs)], 0, "e4m3")
    y = unpack_fp4(w1_words, w1_scales).T @ xq
    yc = y[:, unstriped(cen)]
    e = unpack_fp4(w2_words, w2_scales).T @ xq
    h = unpack_fp4(w3_words, w3_scales).T @ xq
    z = (sigmoid(yc + e[:, unstriped(pos1)])) * h[:, unstriped(pos1)] + (sigmoid(yc + e[:, unstriped(pos2)])) * h[:, unstriped(pos2)] + (sigmoid(yc + e[:, unstriped(pos3)])) * h[:, unstriped(pos3)]
    return z

@@ -1,0 +1,143 @@
+from contextlib import ExitStack
+
+import concourse.mybir as mybir
+
+K, T, S, V, N = 1024, 2048, 512, 256, 128
+FLOPS = 3 * 2 * K * S * N
+
+F32 = mybir.dt.float32
+BF16 = mybir.dt.bfloat16
+I32 = mybir.dt.int32
+U32 = mybir.dt.uint32
+U16 = mybir.dt.uint16
+U8 = mybir.dt.uint8
+FP8X4 = mybir.dt.float8_e4m3fn_x4
+FP4X4 = mybir.dt.float4_e2m1fn_x4
+ADD = mybir.AluOpType.add
+MULT = mybir.AluOpType.mult
+SIGMOID = mybir.ActivationFunctionType.Sigmoid
+
+P = 128
+PACK = 4
+K_PASS = P * PACK
+PASSES = K // K_PASS
+HALF = S // 2
+QUARTER = S // 4
+VH = V // 2
+
+
+def tile_picked_gatedg_none_e_kernel(tc, xT, w1_words, w1_scales, w2_words, w2_scales, w3_words, w3_scales, offs, cen, pos1, pos2, pos3, out):
+    nc = tc.nc
+    with ExitStack() as ctx:
+        keep = ctx.enter_context(tc.tile_pool(name="keep", bufs=1))
+        psum = ctx.enter_context(tc.psum_pool(name="psum", bufs=1))
+
+        def load_list(name, src):
+            tile = keep.tile(list(src.shape), U16, name=name)
+            nc.sync.dma_start(tile[:], src)
+            return tile
+
+        def load_plane(z, j):
+            tile = keep.tile([P, T], F32, name="plane%d%d" % (z, j))
+            rows = xT[z * K_PASS : (z + 1) * K_PASS, :].rearrange("(p j) t -> p j t", j=PACK)
+            nc.sync.dma_start(tile[:], rows[:, j, :])
+            return tile
+
+        def load_words(name, src):
+            tile = keep.tile([P, PASSES, 2 * N], U8, name=name, align_bytes=64)
+            nc.sync.dma_start(tile[:].bitcast(I32), src.rearrange("z p c -> p z c").bitcast(I32))
+            return tile
+
+        def load_scales(name, src):
+            tile = keep.tile([P, PASSES, N], U8, name=name, align_bytes=64)
+            nc.gpsimd.memset(tile[:].bitcast(I32), 0)
+            for q in range(4):
+                nc.gpsimd.dma_start(
+                    tile[32 * q : 32 * q + 4, :, :].bitcast(I32),
+                    src[:, 4 * q : 4 * q + 4, :].rearrange("z r c -> r z c").bitcast(I32),
+                )
+            return tile
+
+        w_scales = [load_scales("ws%d" % m, src) for m, src in enumerate((w1_scales, w2_scales, w3_scales))]
+
+        planes = {(0, 0): load_plane(0, 0)}
+        offs_t = load_list("offs_t", offs)
+        for z in range(PASSES):
+            for j in range(PACK):
+                if (z, j) != (0, 0):
+                    planes[(z, j)] = load_plane(z, j)
+        w_words = [load_words("ww%d" % m, src) for m, src in enumerate((w1_words, w2_words, w3_words))]
+        cen_t = load_list("cen_t", cen)
+        pos_t = [load_list("pos_t%d" % d, src) for d, src in enumerate((pos1, pos2, pos3))]
+
+        codes = [keep.tile([P, S], U32, name="codes%d" % z, align_bytes=64) for z in range(PASSES)]
+        scales = [keep.tile([P, S], U8, name="scales%d" % z, align_bytes=64) for z in range(PASSES)]
+
+        for z in range(PASSES):
+            grouped = [keep.tile([P, HALF, PACK], BF16, name="grouped%d%d" % (z, a), align_bytes=64) for a in range(2)]
+            for j in range(PACK):
+                for a in range(2):
+                    cols = slice(a * HALF // 16, (a + 1) * HALF // 16)
+                    nc.vector.tensor_copy(grouped[a][:, :, j], planes[(z, j)][:].indirect(offs_t[:, cols]))
+            for a in range(2):
+                nodes = slice(a * HALF, (a + 1) * HALF)
+                nc.vector.quantize_mx(
+                    out=codes[z][:, nodes].bitcast(FP8X4),
+                    scales=scales[z][:, nodes],
+                    in_=grouped[a][:].rearrange("p s j -> p (s j)"),
+                )
+
+        def product(acc, m, z, nodes):
+            nc.tensor.matmul_mx(
+                out=acc[:],
+                lhsT=w_words[m][:, z, :].bitcast(FP4X4),
+                lhsT_scale=w_scales[m][:, z, :],
+                rhs=codes[z][:, nodes].bitcast(FP8X4),
+                rhs_scale=scales[z][:, nodes],
+                start=(z == 0),
+                stop=(z == PASSES - 1),
+            )
+
+        y_acc = [psum.tile([P, QUARTER], F32, name="y_acc%d" % q) for q in range(4)]
+        e_acc = psum.tile([P, S], F32, name="e_acc")
+        h_acc = psum.tile([P, S], F32, name="h_acc")
+        for z in range(PASSES):
+            for q in range(4):
+                product(y_acc[q], 0, z, slice(q * QUARTER, (q + 1) * QUARTER))
+            product(e_acc, 1, z, slice(0, S))
+            product(h_acc, 2, z, slice(0, S))
+
+        y = keep.tile([P, S], F32, name="y")
+        e = keep.tile([P, S], F32, name="e")
+        h = keep.tile([P, S], F32, name="h")
+        for q in range(4):
+            dst = y[:, q * QUARTER : (q + 1) * QUARTER]
+            if q == 2:
+                nc.vector.tensor_copy(dst, y_acc[q][:])
+            else:
+                nc.scalar.copy(dst, y_acc[q][:])
+        nc.scalar.copy(e[:], e_acc[:])
+        nc.scalar.copy(h[:], h_acc[:])
+
+        yc = keep.tile([P, V], F32, name="yc")
+        nc.vector.tensor_copy(yc[:], y[:].indirect(cen_t[:]))
+        gate = []
+        for d in range(3):
+            u = keep.tile([P, V], F32, name="u%d" % d)
+            nc.vector.tensor_tensor(u[:], e[:].indirect(pos_t[d][:]), yc[:], ADD)
+            g = keep.tile([P, V], F32, name="g%d" % d)
+            nc.scalar.activation(g[:], u[:], SIGMOID)
+            gate.append(g)
+        msg = [keep.tile([P, V], F32, name="msg%d" % d) for d in range(2)]
+        for d in range(2):
+            nc.vector.tensor_tensor(msg[d][:], h[:].indirect(pos_t[d][:]), gate[d][:], MULT)
+        last = [keep.tile([P, VH], F32, name="last%d" % a) for a in range(2)]
+        res = [keep.tile([P, VH], F32, name="res%d" % a) for a in range(2)]
+        both = keep.tile([P, V], F32, name="both")
+        nc.vector.tensor_tensor(last[0][:], h[:].indirect(pos_t[2][:, 0 : VH // 16]), gate[2][:, 0:VH], MULT)
+        nc.vector.tensor_tensor(both[:], msg[0][:], msg[1][:], ADD)
+        nc.vector.tensor_tensor(last[1][:], h[:].indirect(pos_t[2][:, VH // 16 : V // 16]), gate[2][:, VH:V], MULT)
+        for a in range(2):
+            cols = slice(a * VH, (a + 1) * VH)
+            nc.vector.tensor_tensor(res[a][:], both[:, cols], last[a][:], ADD)
+            nc.sync.dma_start(out[:, cols], res[a][:])

@@ -48,27 +48,33 @@ def tile_picked_gatedg_none_e_kernel(tc, xT, w1_words, w1_scales, w2_words, w2_s
             nc.sync.dma_start(tile[:].bitcast(I32), src.rearrange("z p c -> p z c").bitcast(I32))
             return tile
 
-        def load_scales(name, src):
-            tile = keep.tile([P, PASSES, N], U8, name=name, align_bytes=64)
-            nc.gpsimd.memset(tile[:].bitcast(I32), 0)
+        w_scales = keep.tile([P, 3, PASSES, N], U8, name="w_scales", align_bytes=64)
+        nc.vector.memset(w_scales[:].bitcast(I32), 0)
+
+        def load_scales(m, src):
             for q in range(4):
-                nc.gpsimd.dma_start(
-                    tile[32 * q : 32 * q + 4, :, :].bitcast(I32),
+                nc.sync.dma_start(
+                    w_scales[32 * q : 32 * q + 4, m, :, :].bitcast(I32),
                     src[:, 4 * q : 4 * q + 4, :].rearrange("z r c -> r z c").bitcast(I32),
                 )
-            return tile
 
-        w_scales = [load_scales("ws%d" % m, src) for m, src in enumerate((w1_scales, w2_scales, w3_scales))]
+        warm_in = keep.tile([P, 1], F32, name="warm_in")
+        warm_out = keep.tile([P, 1], F32, name="warm_out")
+        nc.gpsimd.memset(warm_in[:], 0.0)
+        nc.scalar.activation(warm_out[:], warm_in[:], SIGMOID)
 
         planes = {(0, 0): load_plane(0, 0)}
         offs_t = load_list("offs_t", offs)
-        for z in range(PASSES):
-            for j in range(PACK):
-                if (z, j) != (0, 0):
-                    planes[(z, j)] = load_plane(z, j)
-        w_words = [load_words("ww%d" % m, src) for m, src in enumerate((w1_words, w2_words, w3_words))]
+        load_scales(0, w1_scales)
+        for i in range(1, PASSES * PACK):
+            planes[divmod(i, PACK)] = load_plane(*divmod(i, PACK))
+        w_words = [load_words("ww0", w1_words), load_words("ww1", w2_words)]
+        load_scales(1, w2_scales)
         cen_t = load_list("cen_t", cen)
-        pos_t = [load_list("pos_t%d" % d, src) for d, src in enumerate((pos1, pos2, pos3))]
+        pos_t = [load_list("pos_t0", pos1)]
+        w_words.append(load_words("ww2", w3_words))
+        load_scales(2, w3_scales)
+        pos_t.extend([load_list("pos_t1", pos2), load_list("pos_t2", pos3)])
 
         codes = [keep.tile([P, S], U32, name="codes%d" % z, align_bytes=64) for z in range(PASSES)]
         scales = [keep.tile([P, S], U8, name="scales%d" % z, align_bytes=64) for z in range(PASSES)]
@@ -91,40 +97,44 @@ def tile_picked_gatedg_none_e_kernel(tc, xT, w1_words, w1_scales, w2_words, w2_s
             nc.tensor.matmul_mx(
                 out=acc[:],
                 lhsT=w_words[m][:, z, :].bitcast(FP4X4),
-                lhsT_scale=w_scales[m][:, z, :],
+                lhsT_scale=w_scales[:, m, z, :],
                 rhs=codes[z][:, nodes].bitcast(FP8X4),
                 rhs_scale=scales[z][:, nodes],
                 start=(z == 0),
                 stop=(z == PASSES - 1),
             )
 
-        y_acc = [psum.tile([P, QUARTER], F32, name="y_acc%d" % q) for q in range(4)]
-        e_acc = psum.tile([P, S], F32, name="e_acc")
-        h_acc = psum.tile([P, S], F32, name="h_acc")
+        acc = [[psum.tile([P, QUARTER], F32, name="acc%d%d" % (m, q), tag="bank%d%d" % (m, q)) for q in range(4)] for m in range(2)]
         for z in range(PASSES):
-            for q in range(4):
-                product(y_acc[q], 0, z, slice(q * QUARTER, (q + 1) * QUARTER))
-            product(e_acc, 1, z, slice(0, S))
-            product(h_acc, 2, z, slice(0, S))
+            for m in range(2):
+                for q in range(4):
+                    product(acc[m][q], m, z, slice(q * QUARTER, (q + 1) * QUARTER))
 
         y = keep.tile([P, S], F32, name="y")
         e = keep.tile([P, S], F32, name="e")
         h = keep.tile([P, S], F32, name="h")
-        for q in range(4):
-            dst = y[:, q * QUARTER : (q + 1) * QUARTER]
-            if q == 2:
-                nc.vector.tensor_copy(dst, y_acc[q][:])
-            else:
-                nc.scalar.copy(dst, y_acc[q][:])
-        nc.scalar.copy(e[:], e_acc[:])
+        for m, full in enumerate((y, e)):
+            for q in range(4):
+                dst = full[:, q * QUARTER : (q + 1) * QUARTER]
+                if (m, q) == (0, 2):
+                    nc.vector.tensor_copy(dst, acc[m][q][:])
+                else:
+                    nc.scalar.copy(dst, acc[m][q][:])
+        h_acc = psum.tile([P, S], F32, name="h_acc", tag="bank00")
+        for z in range(PASSES):
+            product(h_acc, 2, z, slice(0, S))
         nc.scalar.copy(h[:], h_acc[:])
 
         yc = keep.tile([P, V], F32, name="yc")
-        nc.vector.tensor_copy(yc[:], y[:].indirect(cen_t[:]))
+        for a in range(2):
+            nc.vector.tensor_copy(yc[:, a * VH : (a + 1) * VH], y[:].indirect(cen_t[:, a * VH // 16 : (a + 1) * VH // 16]))
         gate = []
         for d in range(3):
             u = keep.tile([P, V], F32, name="u%d" % d)
-            nc.vector.tensor_tensor(u[:], e[:].indirect(pos_t[d][:]), yc[:], ADD)
+            pieces = 2 if d == 0 else 1
+            for a in range(pieces):
+                cols = slice(a * V // pieces, (a + 1) * V // pieces)
+                nc.vector.tensor_tensor(u[:, cols], e[:].indirect(pos_t[d][:, cols.start // 16 : cols.stop // 16]), yc[:, cols], ADD)
             g = keep.tile([P, V], F32, name="g%d" % d)
             nc.scalar.activation(g[:], u[:], SIGMOID)
             gate.append(g)

@@ -81,10 +81,13 @@ def tile_picked_gatedg_none_e_kernel(tc, xT, w1_words, w1_scales, w2_words, w2_s
 
         for z in range(PASSES):
             grouped = [keep.tile([P, HALF, PACK], BF16, name="grouped%d%d" % (z, a), align_bytes=64) for a in range(2)]
+            pair = keep.tile([P, 2, HALF], BF16, name="pair%d" % z)
             for j in range(PACK):
-                for a in range(2):
-                    cols = slice(a * HALF // 16, (a + 1) * HALF // 16)
-                    nc.vector.tensor_copy(grouped[a][:, :, j], planes[(z, j)][:].indirect(offs_t[:, cols]))
+                window = planes[(z, j)]
+                nc.vector.tensor_copy(pair[:, j, :] if j < 2 else grouped[0][:, :, j], window[:].indirect(offs_t[:, 0 : HALF // 16]))
+                nc.vector.tensor_copy(grouped[1][:, :, j], window[:].indirect(offs_t[:, HALF // 16 : S // 16]))
+                if j == 1:
+                    nc.scalar.copy(grouped[0][:, :, 0:2], pair[:].rearrange("p j s -> p s j"))
             for a in range(2):
                 nodes = slice(a * HALF, (a + 1) * HALF)
                 nc.vector.quantize_mx(

from contextlib import ExitStack

import concourse.mybir as mybir

K, T, S, V, N = 1024, 2048, 512, 256, 128
FLOPS = 3 * 2 * K * S * N

F32 = mybir.dt.float32
BF16 = mybir.dt.bfloat16
I32 = mybir.dt.int32
U32 = mybir.dt.uint32
U16 = mybir.dt.uint16
U8 = mybir.dt.uint8
FP8X4 = mybir.dt.float8_e4m3fn_x4
FP4X4 = mybir.dt.float4_e2m1fn_x4
ADD = mybir.AluOpType.add
MULT = mybir.AluOpType.mult
SIGMOID = mybir.ActivationFunctionType.Sigmoid

P = 128
PACK = 4
K_PASS = P * PACK
PASSES = K // K_PASS
HALF = S // 2
QUARTER = S // 4
VH = V // 2


def tile_picked_gatedg_none_e_kernel(tc, xT, w1_words, w1_scales, w2_words, w2_scales, w3_words, w3_scales, offs, cen, pos1, pos2, pos3, out):
    nc = tc.nc
    with ExitStack() as ctx:
        keep = ctx.enter_context(tc.tile_pool(name="keep", bufs=1))
        psum = ctx.enter_context(tc.psum_pool(name="psum", bufs=1))

        def load_list(name, src):
            tile = keep.tile(list(src.shape), U16, name=name)
            nc.sync.dma_start(tile[:], src)
            return tile

        def load_plane(z, j):
            tile = keep.tile([P, T], F32, name="plane%d%d" % (z, j))
            rows = xT[z * K_PASS : (z + 1) * K_PASS, :].rearrange("(p j) t -> p j t", j=PACK)
            nc.sync.dma_start(tile[:], rows[:, j, :])
            return tile

        def load_words(name, src):
            tile = keep.tile([P, PASSES, 2 * N], U8, name=name, align_bytes=64)
            nc.sync.dma_start(tile[:].bitcast(I32), src.rearrange("z p c -> p z c").bitcast(I32))
            return tile

        w_scales = keep.tile([P, 3, PASSES, N], U8, name="w_scales", align_bytes=64)
        nc.vector.memset(w_scales[:].bitcast(I32), 0)

        def load_scales(m, src):
            for q in range(4):
                nc.sync.dma_start(
                    w_scales[32 * q : 32 * q + 4, m, :, :].bitcast(I32),
                    src[:, 4 * q : 4 * q + 4, :].rearrange("z r c -> r z c").bitcast(I32),
                )

        warm_in = keep.tile([P, 1], F32, name="warm_in")
        warm_out = keep.tile([P, 1], F32, name="warm_out")
        nc.gpsimd.memset(warm_in[:], 0.0)
        nc.scalar.activation(warm_out[:], warm_in[:], SIGMOID)

        planes = {(0, 0): load_plane(0, 0)}
        offs_t = load_list("offs_t", offs)
        load_scales(0, w1_scales)
        for i in range(1, PASSES * PACK):
            planes[divmod(i, PACK)] = load_plane(*divmod(i, PACK))
        w_words = [load_words("ww0", w1_words), load_words("ww1", w2_words)]
        load_scales(1, w2_scales)
        cen_t = load_list("cen_t", cen)
        pos_t = [load_list("pos_t0", pos1)]
        w_words.append(load_words("ww2", w3_words))
        load_scales(2, w3_scales)
        pos_t.extend([load_list("pos_t1", pos2), load_list("pos_t2", pos3)])

        codes = [keep.tile([P, S], U32, name="codes%d" % z, align_bytes=64) for z in range(PASSES)]
        scales = [keep.tile([P, S], U8, name="scales%d" % z, align_bytes=64) for z in range(PASSES)]

        for z in range(PASSES):
            grouped = [keep.tile([P, HALF, PACK], BF16, name="grouped%d%d" % (z, a), align_bytes=64) for a in range(2)]
            pair = keep.tile([P, 2, HALF], BF16, name="pair%d" % z)
            for j in range(PACK):
                window = planes[(z, j)]
                nc.vector.tensor_copy(pair[:, j, :] if j < 2 else grouped[0][:, :, j], window[:].indirect(offs_t[:, 0 : HALF // 16]))
                nc.vector.tensor_copy(grouped[1][:, :, j], window[:].indirect(offs_t[:, HALF // 16 : S // 16]))
                if j == 1:
                    nc.scalar.copy(grouped[0][:, :, 0:2], pair[:].rearrange("p j s -> p s j"))
            for a in range(2):
                nodes = slice(a * HALF, (a + 1) * HALF)
                nc.vector.quantize_mx(
                    out=codes[z][:, nodes].bitcast(FP8X4),
                    scales=scales[z][:, nodes],
                    in_=grouped[a][:].rearrange("p s j -> p (s j)"),
                )

        def product(acc, m, z, nodes):
            nc.tensor.matmul_mx(
                out=acc[:],
                lhsT=w_words[m][:, z, :].bitcast(FP4X4),
                lhsT_scale=w_scales[:, m, z, :],
                rhs=codes[z][:, nodes].bitcast(FP8X4),
                rhs_scale=scales[z][:, nodes],
                start=(z == 0),
                stop=(z == PASSES - 1),
            )

        acc = [[psum.tile([P, QUARTER], F32, name="acc%d%d" % (m, q), tag="bank%d%d" % (m, q)) for q in range(4)] for m in range(2)]
        for z in range(PASSES):
            for m in range(2):
                for q in range(4):
                    product(acc[m][q], m, z, slice(q * QUARTER, (q + 1) * QUARTER))

        y = keep.tile([P, S], F32, name="y")
        e = keep.tile([P, S], F32, name="e")
        h = keep.tile([P, S], F32, name="h")
        for m, full in enumerate((y, e)):
            for q in range(4):
                dst = full[:, q * QUARTER : (q + 1) * QUARTER]
                if (m, q) == (0, 2):
                    nc.vector.tensor_copy(dst, acc[m][q][:])
                else:
                    nc.scalar.copy(dst, acc[m][q][:])
        h_acc = psum.tile([P, S], F32, name="h_acc", tag="bank00")
        for z in range(PASSES):
            product(h_acc, 2, z, slice(0, S))
        nc.scalar.copy(h[:], h_acc[:])

        yc = keep.tile([P, V], F32, name="yc")
        for a in range(2):
            nc.vector.tensor_copy(yc[:, a * VH : (a + 1) * VH], y[:].indirect(cen_t[:, a * VH // 16 : (a + 1) * VH // 16]))
        gate = []
        for d in range(3):
            u = keep.tile([P, V], F32, name="u%d" % d)
            pieces = 2 if d == 0 else 1
            for a in range(pieces):
                cols = slice(a * V // pieces, (a + 1) * V // pieces)
                nc.vector.tensor_tensor(u[:, cols], e[:].indirect(pos_t[d][:, cols.start // 16 : cols.stop // 16]), yc[:, cols], ADD)
            g = keep.tile([P, V], F32, name="g%d" % d)
            nc.scalar.activation(g[:], u[:], SIGMOID)
            gate.append(g)
        msg = [keep.tile([P, V], F32, name="msg%d" % d) for d in range(2)]
        for d in range(2):
            nc.vector.tensor_tensor(msg[d][:], h[:].indirect(pos_t[d][:]), gate[d][:], MULT)
        last = [keep.tile([P, VH], F32, name="last%d" % a) for a in range(2)]
        res = [keep.tile([P, VH], F32, name="res%d" % a) for a in range(2)]
        both = keep.tile([P, V], F32, name="both")
        nc.vector.tensor_tensor(last[0][:], h[:].indirect(pos_t[2][:, 0 : VH // 16]), gate[2][:, 0:VH], MULT)
        nc.vector.tensor_tensor(both[:], msg[0][:], msg[1][:], ADD)
        nc.vector.tensor_tensor(last[1][:], h[:].indirect(pos_t[2][:, VH // 16 : V // 16]), gate[2][:, VH:V], MULT)
        for a in range(2):
            cols = slice(a * VH, (a + 1) * VH)
            nc.vector.tensor_tensor(res[a][:], both[:, cols], last[a][:], ADD)
            nc.sync.dma_start(out[:, cols], res[a][:])
